import numpy as np
import ml_dtypes


def mxq(x, axis, fmt="e4m3"):
    dtype, down = {"e4m3": (ml_dtypes.float8_e4m3fn, 7), "e5m2": (ml_dtypes.float8_e5m2, 14)}[fmt]
    v = np.moveaxis(np.asarray(x, np.float32).astype(ml_dtypes.bfloat16).astype(np.float64), axis, -1)
    blocks = v.reshape(v.shape[:-1] + (-1, 32))
    amax = np.abs(blocks).max(-1, keepdims=True)
    byte = np.maximum(np.where(amax > 0, np.frexp(amax)[1] - 1 + 127, 0) - down, 1)
    scale = np.exp2(byte - 127.0)
    codes = (blocks / scale).astype(np.float32).astype(dtype).astype(np.float64)
    return np.moveaxis((codes * scale).reshape(v.shape), -1, axis)


WIDE = False


def mx_kscale(k):
    if not WIDE:
        return np.ones(k)
    levels = np.array([10, -10, 5, -5, 0])
    if k % 512:
        return np.exp2(np.random.permutation(np.resize(levels, k // 32))).repeat(32)
    a = np.empty((k // 512, 16))
    for p in range(k // 512):
        a[p, :8] = np.random.permutation(np.resize(levels, 8))
        for g in range(8):
            far = levels[np.abs(levels - a[p, g]) >= 10]
            a[p, g + 8] = far[np.random.randint(len(far))]
    return np.exp2(a.ravel()).repeat(32)


def f64(x):
    return np.asarray(x).astype(np.float64)


def striped(idx):
    return np.tile(idx.reshape(-1, 16).T, (8, 1)).astype(np.uint16)


def unstriped(offs):
    return offs[:16].T.reshape(-1).astype(np.int64)


def gelu(v):
    return 0.5 * v * (1.0 + np.tanh(np.sqrt(2.0 / np.pi) * (v + 0.044715 * v**3)))


K, T, E, C, H, N = 1536, 1536, 4, 128, 512, 128


def by_expert(wq, xq):
    return np.concatenate([wq[e].T @ xq[:, e * C:(e + 1) * C] for e in range(E)], axis=1)


def setup_inputs():
    n = np.random.standard_normal
    s = mx_kscale(K)[:, None]
    u = mx_kscale(H)
    return {
        "xT": (n((K, T)) * s).astype(np.float32),
        "w1": (n((E, K, H)) / np.sqrt(K) / s[None] * u[None, None, :]).astype(np.float32),
        "w2": (n((E, H, N)) / np.sqrt(H) / u[None, :, None]).astype(np.float32),
        "gate": np.tile(np.random.uniform(0.2, 1.0, E * C), (N, 1)).astype(np.float32),
        "offs": striped(np.random.permutation(T)[:E * C]),
    }


def reference(xT, w1, w2, gate, offs):
    idx = unstriped(offs)
    xq = mxq(f64(xT)[:, idx], 0, "e4m3")
    h = gelu(by_expert(mxq(f64(w1), 1, "e4m3"), xq))
    y = by_expert(mxq(f64(w2), 1, "e4m3"), mxq(h, 0, "e4m3"))
    out = np.zeros((N, T))
    out[:, idx] = f64(gate) * y
    return out

@@ -1,0 +1,294 @@
+from contextlib import ExitStack
+
+import concourse.mybir as mybir
+
+K, T, E, C, H, N = 1536, 1536, 4, 128, 512, 128
+SLOTS = E * C
+P = 128
+PACK = 4
+K_PASS = P * PACK
+PASSES = K // K_PASS
+FLOPS = 2 * SLOTS * (K * H + H * N)
+
+F32 = mybir.dt.float32
+BF16 = mybir.dt.bfloat16
+U32 = mybir.dt.uint32
+U16 = mybir.dt.uint16
+U8 = mybir.dt.uint8
+FP8X4 = mybir.dt.float8_e4m3fn_x4
+GELU = mybir.ActivationFunctionType.Gelu_apprx_tanh
+MULT = mybir.AluOpType.mult
+
+
+def tile_routed_moe_kernel(tc, xT, w1, w2, gate, offs, out):
+    nc = tc.nc
+    with ExitStack() as ctx:
+        keep = ctx.enter_context(tc.tile_pool(name="keep", bufs=1))
+        raws = ctx.enter_context(tc.tile_pool(name="raws", bufs=2))
+        work = ctx.enter_context(tc.tile_pool(name="work", bufs=2))
+        psum = ctx.enter_context(tc.psum_pool(name="psum", bufs=1))
+
+        offsets = keep.tile([P, SLOTS // 16], U16, name="offsets")
+        nc.sync.dma_start(offsets[:], offs)
+
+        x_raw, w1_raw = {}, {}
+        w2_raw = keep.tile([P, E, PACK * N], F32, name="w2_raw")
+        gates = keep.tile([P, SLOTS], F32, name="gates")
+        w1_passes = w1.rearrange("e (s p j) c -> p (e s) (j c)", p=P, j=PACK)
+
+        def load_x(s, width):
+            x_raw[s] = raws.tile([P, PACK * T], F32, name=f"x_raw{s}", tag="x_raw", bufs=3)
+            rows = xT[s * K_PASS:(s + 1) * K_PASS, :].rearrange("(p j) n -> p (j n)", j=PACK)
+            for j in range(0, PACK, width):
+                cols = slice(j * T, (j + width) * T)
+                nc.sync.dma_start(out=x_raw[s][:, cols], in_=rows[:, cols])
+
+        def load_w2(first, last):
+            nc.sync.dma_start(out=w2_raw[:, first:last, :], in_=w2[first:last].rearrange("e (p j) n -> p e (j n)", j=PACK))
+
+        def load_gate(a, b):
+            nc.sync.dma_start(out=gates[:, a:b], in_=gate[:, a:b])
+
+        def load_w1(ks, bufs):
+            raw = raws.tile([P, len(ks), PACK * H], F32, name=f"w1_raw{ks[0]}", tag=f"w1_raw{len(ks)}", bufs=bufs)
+            nc.sync.dma_start(out=raw[:], in_=w1_passes[:, ks[0]:ks[-1] + 1, :])
+            for i, k in enumerate(ks):
+                w1_raw[k] = raw[:, i, :]
+
+        load_x(0, 1)
+        load_x(1, 1)
+        load_x(2, 1)
+        load_w2(0, 2)
+        load_gate(0, 256)
+        load_w1((0,), 8)
+        load_w1((1,), 8)
+        load_w1((2,), 8)
+        load_w1((3,), 8)
+        load_w1((4,), 8)
+        load_w1((5,), 8)
+        load_w1((6,), 8)
+        load_w1((7,), 8)
+        load_w1((8,), 8)
+        load_w1((9,), 8)
+        load_w1((10,), 8)
+        load_w1((11,), 8)
+        load_w2(2, 4)
+        load_gate(256, 512)
+
+        window = keep.tile([P, T], F32, name="window")
+        nc.gpsimd.memset(window[:], 0.0)
+        warm = keep.tile([P, 1], F32, name="warm")
+        nc.gpsimd.memset(warm[:], 0.0)
+        nc.scalar.activation(warm[:], warm[:], GELU)
+
+        x_codes = keep.tile([P, PASSES, SLOTS], U32, name="x_codes", align_bytes=64)
+        x_scales = keep.tile([P, PASSES, SLOTS], U8, name="x_scales", align_bytes=64)
+        picked, x_grouped = {}, {}
+
+        def gather(s):
+            picked[s] = work.tile([P, PACK, SLOTS], F32, name=f"picked{s}", tag="picked")
+            for j in range(PACK):
+                nc.vector.tensor_copy(picked[s][:, j, :], x_raw[s][:, j * T:(j + 1) * T].indirect(offsets[:]))
+
+        def group_tokens(s):
+            x_grouped[s] = work.tile([P, SLOTS * PACK], BF16, name=f"x_grouped{s}", tag="x_grouped", align_bytes=64)
+            nc.scalar.copy(
+                out=x_grouped[s][:].rearrange("p (c i j) -> p c j i", i=4, j=PACK),
+                in_=picked[s][:].rearrange("p j (c i) -> p c j i", i=4),
+            )
+
+        def quantize_tokens(s):
+            nc.vector.quantize_mx(out=x_codes[:, s, :].bitcast(FP8X4), scales=x_scales[:, s, :], in_=x_grouped[s][:])
+
+        w2_codes = keep.tile([P, E, N], U32, name="w2_codes", align_bytes=64)
+        w2_scales = keep.tile([P, E, N], U8, name="w2_scales", align_bytes=64)
+        w2_grouped = keep.tile([P, E, N * PACK], BF16, name="w2_grouped", align_bytes=64)
+
+        def group_w2(first, last):
+            nc.scalar.copy(
+                out=w2_grouped[:, first:last, :].rearrange("p e (c i j) -> p e c j i", i=4, j=PACK),
+                in_=w2_raw[:, first:last, :].rearrange("p e (j c i) -> p e c j i", i=4, j=PACK),
+            )
+
+        def quantize_w2(first, last):
+            nc.vector.quantize_mx(
+                out=w2_codes[:, first:last, :].rearrange("p e n -> p (e n)").bitcast(FP8X4),
+                scales=w2_scales[:, first:last, :].rearrange("p e n -> p (e n)"),
+                in_=w2_grouped[:, first:last, :].rearrange("p e f -> p (e f)"),
+            )
+
+        y_all = keep.tile([P, SLOTS], F32, name="y_all")
+        w1_codes, w1_scales, w1_grouped, sums, ys = {}, {}, {}, {}, {}
+
+        def copy_w1(copy, grouped, k, m, t):
+            if m.start < m.stop:
+                copy(
+                    out=grouped[:].rearrange("p (t m j) -> p m j t", t=4, j=PACK)[:, m, :, t],
+                    in_=w1_raw[k].rearrange("p (j m t) -> p m j t", j=PACK, t=4)[:, m, :, t],
+                )
+
+        def group_w1(k, cut, halves):
+            grouped = work.tile([P, H * PACK], BF16, name=f"w1_grouped{k}", tag=f"slot{k % 4}", align_bytes=64, bufs=1)
+            w1_grouped[k] = grouped
+            for t in (slice(0, 2), slice(2, 4)) if halves else (slice(0, 4),):
+                copy_w1(nc.scalar.copy, grouped, k, slice(0, cut), t)
+                copy_w1(nc.vector.tensor_copy, grouped, k, slice(cut, P), t)
+
+        def quantize_w1(k, halves):
+            e, s = divmod(k, PASSES)
+            if s == 0:
+                w1_codes[e] = work.tile([P, PASSES, H], U32, name=f"w1_codes{e}", tag="w1_codes", align_bytes=64)
+                w1_scales[e] = work.tile([P, PASSES, H], U8, name=f"w1_scales{e}", tag="w1_scales", align_bytes=64)
+            width = H // 2 if halves else H
+            for c in range(0, H, width):
+                cols = slice(c, c + width)
+                nc.vector.quantize_mx(
+                    out=w1_codes[e][:, s, cols].bitcast(FP8X4),
+                    scales=w1_scales[e][:, s, cols],
+                    in_=w1_grouped[k][:, c * PACK:(c + width) * PACK],
+                )
+
+        def pass_w1(e, s, t):
+            cols, slots = slice(t * P, (t + 1) * P), slice(e * C, (e + 1) * C)
+            nc.tensor.matmul_mx(
+                out=sums[e, t // 2][:, t % 2, :],
+                lhsT=w1_codes[e][:, s, cols].bitcast(FP8X4),
+                lhsT_scale=w1_scales[e][:, s, cols],
+                rhs=x_codes[:, s, slots].bitcast(FP8X4),
+                rhs_scale=x_scales[:, s, slots],
+                start=(s == 0),
+                stop=(s == PASSES - 1),
+            )
+
+        banks = {}
+
+        def multiply_w1(k):
+            e, s = divmod(k, PASSES)
+            for q in range(2):
+                if s == 0:
+                    if False and e < 2:
+                        if e == 0:
+                            banks[q] = psum.tile([P, 2, 2, C], F32, name=f"acc_pair{q}")
+                        sums[e, q] = banks[q][:, e]
+                    else:
+                        sums[e, q] = psum.tile([P, 2, C], F32, name=f"acc{e}{q}", tag=f"acc{e % 2}{q}")
+                pass_w1(e, s, 2 * q)
+                if s == PASSES - 1:
+                    for r in range(PASSES):
+                        pass_w1(e, r, 2 * q + 1)
+
+        hidden = {}
+
+        def hidden_in(slot, pair):
+            if slot is None:
+                hidden[pair] = keep.tile([P, 2, C * 4], BF16, name=f"hidden{pair}", align_bytes=64)
+            else:
+                hidden[pair] = work.tile([P, 2, C * 4], BF16, name=f"hidden{pair}", tag=f"slot{slot % 4}", align_bytes=64, bufs=1)
+
+        def apply_gelu(e):
+            for q in range(2):
+                if False and e < 2:
+                    if e == 1:
+                        nc.scalar.activation(
+                            hidden[0][:].rearrange("p e (n q t) -> p q e n t", q=2, t=2)[:, q],
+                            banks[q][:].rearrange("p e t n -> p e n t"),
+                            GELU,
+                        )
+                else:
+                    nc.scalar.activation(
+                        hidden[e // 2][:, e % 2, :].rearrange("p (n q t) -> p q n t", q=2, t=2)[:, q],
+                        sums[e, q][:].rearrange("p t n -> p n t"),
+                        GELU,
+                    )
+
+        def multiply_w2(first, last):
+            count = last - first
+            h_codes = keep.tile([P, count, C], U32, name=f"h_codes{first}", align_bytes=64)
+            h_scales = keep.tile([P, count, C], U8, name=f"h_scales{first}", align_bytes=64)
+            nc.vector.quantize_mx(
+                out=h_codes[:].rearrange("p e c -> p (e c)").bitcast(FP8X4),
+                scales=h_scales[:].rearrange("p e c -> p (e c)"),
+                in_=hidden[first // 2][:, first % 2:first % 2 + count, :].rearrange("p e f -> p (e f)"),
+            )
+            ys[first] = psum.tile([P, count, C], F32, name=f"y{first}", tag=f"y{(first + 1) // 2 % 2}")
+            for e in range(first, last):
+                nc.tensor.matmul_mx(
+                    out=ys[first][:, e - first, :],
+                    lhsT=w2_codes[:, e, :].bitcast(FP8X4),
+                    lhsT_scale=w2_scales[:, e, :],
+                    rhs=h_codes[:, e - first, :].bitcast(FP8X4),
+                    rhs_scale=h_scales[:, e - first, :],
+                    start=True,
+                    stop=True,
+                )
+
+        def take_out(first, last):
+            nc.scalar.copy(y_all[:, first * C:last * C], ys[first][:].rearrange("p e c -> p (e c)"))
+
+        def put_back(a, b):
+            nc.vector.tensor_tensor(
+                window[:].indirect(offsets[:, a // 16:b // 16]), y_all[:, a:b], gates[:, a:b], MULT
+            )
+
+        gather(0)
+        group_tokens(0)
+        quantize_tokens(0)
+        gather(1)
+        group_tokens(1)
+        quantize_tokens(1)
+        gather(2)
+        group_tokens(2)
+        quantize_tokens(2)
+        group_w2(0, 2)
+        quantize_w2(0, 2)
+        group_w1(0, 48, False)
+        quantize_w1(0, False)
+        multiply_w1(0)
+        group_w1(1, 64, False)
+        quantize_w1(1, False)
+        multiply_w1(1)
+        group_w1(2, 96, False)
+        quantize_w1(2, False)
+        multiply_w1(2)
+        group_w1(3, 0, False)
+        quantize_w1(3, False)
+        multiply_w1(3)
+        group_w1(4, 64, False)
+        quantize_w1(4, False)
+        multiply_w1(4)
+        hidden_in(None, 0)
+        apply_gelu(0)
+        group_w1(5, 96, False)
+        quantize_w1(5, False)
+        multiply_w1(5)
+        group_w1(6, 0, False)
+        quantize_w1(6, False)
+        multiply_w1(6)
+        group_w1(7, 64, False)
+        quantize_w1(7, False)
+        multiply_w1(7)
+        apply_gelu(1)
+        multiply_w2(0, 2)
+        take_out(0, 2)
+        group_w1(8, 96, False)
+        quantize_w1(8, False)
+        multiply_w1(8)
+        put_back(0, 256)
+        group_w1(9, 0, False)
+        quantize_w1(9, False)
+        multiply_w1(9)
+        group_w1(10, 64, False)
+        quantize_w1(10, False)
+        multiply_w1(10)
+        hidden_in(None, 1)
+        apply_gelu(2)
+        group_w1(11, 56, False)
+        quantize_w1(11, False)
+        multiply_w1(11)
+        group_w2(2, 4)
+        quantize_w2(2, 4)
+        apply_gelu(3)
+        multiply_w2(2, 4)
+        take_out(2, 4)
+        put_back(256, 512)
+        nc.sync.dma_start(out=out, in_=window[:])

@@ -9,6 +9,10 @@ PACK = 4
 K_PASS = P * PACK
 PASSES = K // K_PASS
 FLOPS = 2 * SLOTS * (K * H + H * N)
+LAST = E - 1
+SCALAR_SHARE = (0, 84, 64)
+SCALAR_SHARE_LAST = 88
+RAW_BUFS = 12
 
 F32 = mybir.dt.float32
 BF16 = mybir.dt.bfloat16
@@ -18,6 +22,7 @@ U8 = mybir.dt.uint8
 FP8X4 = mybir.dt.float8_e4m3fn_x4
 GELU = mybir.ActivationFunctionType.Gelu_apprx_tanh
 MULT = mybir.AluOpType.mult
+ADD = mybir.AluOpType.add
 
 
 def tile_routed_moe_kernel(tc, xT, w1, w2, gate, offs, out):
@@ -34,119 +39,74 @@ def tile_routed_moe_kernel(tc, xT, w1, w2, gate, offs, out):
         x_raw, w1_raw = {}, {}
         w2_raw = keep.tile([P, E, PACK * N], F32, name="w2_raw")
         gates = keep.tile([P, SLOTS], F32, name="gates")
-        w1_passes = w1.rearrange("e (s p j) c -> p (e s) (j c)", p=P, j=PACK)
 
-        def load_x(s, width):
-            x_raw[s] = raws.tile([P, PACK * T], F32, name=f"x_raw{s}", tag="x_raw", bufs=3)
-            rows = xT[s * K_PASS:(s + 1) * K_PASS, :].rearrange("(p j) n -> p (j n)", j=PACK)
-            for j in range(0, PACK, width):
-                cols = slice(j * T, (j + width) * T)
-                nc.sync.dma_start(out=x_raw[s][:, cols], in_=rows[:, cols])
+        def load_x(s):
+            rows = xT[s * K_PASS:(s + 1) * K_PASS, :].rearrange("(p j) n -> p j n", j=PACK)
+            for j in range(PACK):
+                x_raw[s, j] = raws.tile([P, T], F32, name=f"x_raw{s}{j}", tag="raw", bufs=RAW_BUFS)
+                nc.sync.dma_start(out=x_raw[s, j][:], in_=rows[:, j, :])
 
-        def load_w2(first, last):
-            nc.sync.dma_start(out=w2_raw[:, first:last, :], in_=w2[first:last].rearrange("e (p j) n -> p e (j n)", j=PACK))
+        def load_w1(e, s):
+            w1_raw[e, s] = raws.tile([P, PACK * H], F32, name=f"w1_raw{e}{s}", tag="raw", bufs=RAW_BUFS)
+            rows = w1[e, s * K_PASS:(s + 1) * K_PASS, :].rearrange("(p j) c -> p (j c)", j=PACK)
+            nc.sync.dma_start(out=w1_raw[e, s][:], in_=rows)
+
+        def load_w2(e):
+            nc.sync.dma_start(out=w2_raw[:, e, :], in_=w2[e].rearrange("(p j) n -> p (j n)", j=PACK))
 
         def load_gate(a, b):
             nc.sync.dma_start(out=gates[:, a:b], in_=gate[:, a:b])
 
-        def load_w1(ks, bufs):
-            raw = raws.tile([P, len(ks), PACK * H], F32, name=f"w1_raw{ks[0]}", tag=f"w1_raw{len(ks)}", bufs=bufs)
-            nc.sync.dma_start(out=raw[:], in_=w1_passes[:, ks[0]:ks[-1] + 1, :])
-            for i, k in enumerate(ks):
-                w1_raw[k] = raw[:, i, :]
-
-        load_x(0, 1)
-        load_x(1, 1)
-        load_x(2, 1)
-        load_w2(0, 2)
-        load_gate(0, 256)
-        load_w1((0,), 8)
-        load_w1((1,), 8)
-        load_w1((2,), 8)
-        load_w1((3,), 8)
-        load_w1((4,), 8)
-        load_w1((5,), 8)
-        load_w1((6,), 8)
-        load_w1((7,), 8)
-        load_w1((8,), 8)
-        load_w1((9,), 8)
-        load_w1((10,), 8)
-        load_w1((11,), 8)
-        load_w2(2, 4)
-        load_gate(256, 512)
+        for s in range(PASSES):
+            load_x(s)
+        for e in range(E):
+            load_w1(e, 0)
+            if e > 0:
+                load_w2(e - 1)
+            load_w1(e, 1)
+            if e > 0:
+                load_gate((e - 1) * C, e * C)
+            load_w1(e, 2)
+        load_w2(LAST)
+        load_gate(LAST * C, SLOTS)
 
         window = keep.tile([P, T], F32, name="window")
         nc.gpsimd.memset(window[:], 0.0)
+        zeros = keep.tile([P, C], F32, name="zeros")
+        nc.gpsimd.memset(zeros[:], 0.0)
         warm = keep.tile([P, 1], F32, name="warm")
         nc.gpsimd.memset(warm[:], 0.0)
         nc.scalar.activation(warm[:], warm[:], GELU)
 
-        x_codes = keep.tile([P, PASSES, SLOTS], U32, name="x_codes", align_bytes=64)
-        x_scales = keep.tile([P, PASSES, SLOTS], U8, name="x_scales", align_bytes=64)
-        picked, x_grouped = {}, {}
+        first_grouped = keep.tile([P, PASSES, 2, SLOTS * PACK], BF16, name="first_grouped", align_bytes=64)
+        first_codes = keep.tile([P, PASSES, 2, SLOTS], U32, name="first_codes", align_bytes=64)
+        first_scales = keep.tile([P, PASSES, 2, SLOTS], U8, name="first_scales", align_bytes=64)
+        x_codes, x_scales = first_codes[:, :, 0, :], first_scales[:, :, 0, :]
 
-        def gather(s):
-            picked[s] = work.tile([P, PACK, SLOTS], F32, name=f"picked{s}", tag="picked")
+        def prepare_tokens(s):
+            picked = work.tile([P, PACK, SLOTS], F32, name=f"picked{s}", tag="picked")
             for j in range(PACK):
-                nc.vector.tensor_copy(picked[s][:, j, :], x_raw[s][:, j * T:(j + 1) * T].indirect(offsets[:]))
-
-        def group_tokens(s):
-            x_grouped[s] = work.tile([P, SLOTS * PACK], BF16, name=f"x_grouped{s}", tag="x_grouped", align_bytes=64)
+                nc.vector.tensor_copy(picked[:, j, :], x_raw[s, j][:].indirect(offsets[:]))
             nc.scalar.copy(
-                out=x_grouped[s][:].rearrange("p (c i j) -> p c j i", i=4, j=PACK),
-                in_=picked[s][:].rearrange("p j (c i) -> p c j i", i=4),
+                out=first_grouped[:, s, 0, :].rearrange("p (c i j) -> p c j i", i=4, j=PACK),
+                in_=picked[:].rearrange("p j (c i) -> p c j i", i=4),
             )
 
-        def quantize_tokens(s):
-            nc.vector.quantize_mx(out=x_codes[:, s, :].bitcast(FP8X4), scales=x_scales[:, s, :], in_=x_grouped[s][:])
+        w1_codes, w1_scales, w1_grouped, sums = {}, {}, {}, {}
 
-        w2_codes = keep.tile([P, E, N], U32, name="w2_codes", align_bytes=64)
-        w2_scales = keep.tile([P, E, N], U8, name="w2_scales", align_bytes=64)
-        w2_grouped = keep.tile([P, E, N * PACK], BF16, name="w2_grouped", align_bytes=64)
-
-        def group_w2(first, last):
-            nc.scalar.copy(
-                out=w2_grouped[:, first:last, :].rearrange("p e (c i j) -> p e c j i", i=4, j=PACK),
-                in_=w2_raw[:, first:last, :].rearrange("p e (j c i) -> p e c j i", i=4, j=PACK),
-            )
-
-        def quantize_w2(first, last):
-            nc.vector.quantize_mx(
-                out=w2_codes[:, first:last, :].rearrange("p e n -> p (e n)").bitcast(FP8X4),
-                scales=w2_scales[:, first:last, :].rearrange("p e n -> p (e n)"),
-                in_=w2_grouped[:, first:last, :].rearrange("p e f -> p (e f)"),
-            )
-
-        y_all = keep.tile([P, SLOTS], F32, name="y_all")
-        w1_codes, w1_scales, w1_grouped, sums, ys = {}, {}, {}, {}, {}
-
-        def copy_w1(copy, grouped, k, m, t):
+        def copy_w1(copy, e, s, m, t):
             if m.start < m.stop:
                 copy(
-                    out=grouped[:].rearrange("p (t m j) -> p m j t", t=4, j=PACK)[:, m, :, t],
-                    in_=w1_raw[k].rearrange("p (j m t) -> p m j t", j=PACK, t=4)[:, m, :, t],
+                    out=w1_grouped[e, s].rearrange("p (t m j) -> p m j t", t=4, j=PACK)[:, m, :, t],
+                    in_=w1_raw[e, s][:].rearrange("p (j m t) -> p m j t", j=PACK, t=4)[:, m, :, t],
                 )
 
-        def group_w1(k, cut, halves):
-            grouped = work.tile([P, H * PACK], BF16, name=f"w1_grouped{k}", tag=f"slot{k % 4}", align_bytes=64, bufs=1)
-            w1_grouped[k] = grouped
-            for t in (slice(0, 2), slice(2, 4)) if halves else (slice(0, 4),):
-                copy_w1(nc.scalar.copy, grouped, k, slice(0, cut), t)
-                copy_w1(nc.vector.tensor_copy, grouped, k, slice(cut, P), t)
-
-        def quantize_w1(k, halves):
-            e, s = divmod(k, PASSES)
-            if s == 0:
-                w1_codes[e] = work.tile([P, PASSES, H], U32, name=f"w1_codes{e}", tag="w1_codes", align_bytes=64)
-                w1_scales[e] = work.tile([P, PASSES, H], U8, name=f"w1_scales{e}", tag="w1_scales", align_bytes=64)
-            width = H // 2 if halves else H
-            for c in range(0, H, width):
-                cols = slice(c, c + width)
-                nc.vector.quantize_mx(
-                    out=w1_codes[e][:, s, cols].bitcast(FP8X4),
-                    scales=w1_scales[e][:, s, cols],
-                    in_=w1_grouped[k][:, c * PACK:(c + width) * PACK],
-                )
+        def quantize_w1(e, s, a, b):
+            nc.vector.quantize_mx(
+                out=w1_codes[e][:, s, a:b].bitcast(FP8X4),
+                scales=w1_scales[e][:, s, a:b],
+                in_=w1_grouped[e, s][:, a * PACK:b * PACK],
+            )
 
         def pass_w1(e, s, t):
             cols, slots = slice(t * P, (t + 1) * P), slice(e * C, (e + 1) * C)
@@ -160,135 +120,100 @@ def tile_routed_moe_kernel(tc, xT, w1, w2, gate, offs, out):
                 stop=(s == PASSES - 1),
             )
 
-        banks = {}
-
-        def multiply_w1(k):
-            e, s = divmod(k, PASSES)
+        def first_layer(e, s):
+            if e == 0:
+                w1_grouped[e, s] = first_grouped[:, s, 1, :]
+                w1_codes[e], w1_scales[e] = first_codes[:, :, 1, :], first_scales[:, :, 1, :]
+            else:
+                grouped = work.tile([P, H * PACK], BF16, name=f"w1_grouped{e}{s}", tag="w1_grouped", align_bytes=64, bufs=4)
+                w1_grouped[e, s] = grouped[:]
+                if s == 0:
+                    codes = work.tile([P, PASSES, H], U32, name=f"w1_codes{e}", tag="w1_codes", align_bytes=64)
+                    scales = work.tile([P, PASSES, H], U8, name=f"w1_scales{e}", tag="w1_scales", align_bytes=64)
+                    w1_codes[e], w1_scales[e] = codes[:], scales[:]
+            if (e, s) == (LAST, PASSES - 1):
+                cut = SCALAR_SHARE_LAST
+                copy_w1(nc.vector.tensor_copy, e, s, slice(0, P), slice(0, 2))
+                copy_w1(nc.scalar.copy, e, s, slice(0, cut), slice(2, 4))
+                copy_w1(nc.vector.tensor_copy, e, s, slice(cut, P), slice(2, 4))
+                quantize_w1(e, s, 0, H // 2)
+                quantize_w1(e, s, H // 2, H)
+            else:
+                cut = SCALAR_SHARE[s]
+                copy_w1(nc.scalar.copy, e, s, slice(0, cut), slice(0, 4))
+                copy_w1(nc.vector.tensor_copy, e, s, slice(cut, P), slice(0, 4))
+                if e == 0:
+                    nc.vector.quantize_mx(
+                        out=first_codes[:, s].rearrange("p a c -> p (a c)").bitcast(FP8X4),
+                        scales=first_scales[:, s].rearrange("p a c -> p (a c)"),
+                        in_=first_grouped[:, s].rearrange("p a f -> p (a f)"),
+                    )
+                else:
+                    quantize_w1(e, s, 0, H)
             for q in range(2):
                 if s == 0:
-                    if False and e < 2:
-                        if e == 0:
-                            banks[q] = psum.tile([P, 2, 2, C], F32, name=f"acc_pair{q}")
-                        sums[e, q] = banks[q][:, e]
-                    else:
-                        sums[e, q] = psum.tile([P, 2, C], F32, name=f"acc{e}{q}", tag=f"acc{e % 2}{q}")
+                    sums[e, q] = psum.tile([P, 2, C], F32, name=f"acc{e}{q}", tag=f"acc{e % 2}{q}")
                 pass_w1(e, s, 2 * q)
                 if s == PASSES - 1:
                     for r in range(PASSES):
                         pass_w1(e, r, 2 * q + 1)
 
-        hidden = {}
-
-        def hidden_in(slot, pair):
-            if slot is None:
-                hidden[pair] = keep.tile([P, 2, C * 4], BF16, name=f"hidden{pair}", align_bytes=64)
-            else:
-                hidden[pair] = work.tile([P, 2, C * 4], BF16, name=f"hidden{pair}", tag=f"slot{slot % 4}", align_bytes=64, bufs=1)
+        second = {}
 
         def apply_gelu(e):
+            second[e] = work.tile([P, 2, C * PACK], BF16, name=f"second{e}", tag="second", align_bytes=64)
             for q in range(2):
-                if False and e < 2:
-                    if e == 1:
-                        nc.scalar.activation(
-                            hidden[0][:].rearrange("p e (n q t) -> p q e n t", q=2, t=2)[:, q],
-                            banks[q][:].rearrange("p e t n -> p e n t"),
-                            GELU,
-                        )
-                else:
-                    nc.scalar.activation(
-                        hidden[e // 2][:, e % 2, :].rearrange("p (n q t) -> p q n t", q=2, t=2)[:, q],
-                        sums[e, q][:].rearrange("p t n -> p n t"),
-                        GELU,
-                    )
-
-        def multiply_w2(first, last):
-            count = last - first
-            h_codes = keep.tile([P, count, C], U32, name=f"h_codes{first}", align_bytes=64)
-            h_scales = keep.tile([P, count, C], U8, name=f"h_scales{first}", align_bytes=64)
-            nc.vector.quantize_mx(
-                out=h_codes[:].rearrange("p e c -> p (e c)").bitcast(FP8X4),
-                scales=h_scales[:].rearrange("p e c -> p (e c)"),
-                in_=hidden[first // 2][:, first % 2:first % 2 + count, :].rearrange("p e f -> p (e f)"),
-            )
-            ys[first] = psum.tile([P, count, C], F32, name=f"y{first}", tag=f"y{(first + 1) // 2 % 2}")
-            for e in range(first, last):
-                nc.tensor.matmul_mx(
-                    out=ys[first][:, e - first, :],
-                    lhsT=w2_codes[:, e, :].bitcast(FP8X4),
-                    lhsT_scale=w2_scales[:, e, :],
-                    rhs=h_codes[:, e - first, :].bitcast(FP8X4),
-                    rhs_scale=h_scales[:, e - first, :],
-                    start=True,
-                    stop=True,
+                nc.scalar.activation(
+                    second[e][:, 0, :].rearrange("p (n q t) -> p q n t", q=2, t=2)[:, q],
+                    sums[e, q][:].rearrange("p t n -> p n t"),
+                    GELU,
                 )
 
-        def take_out(first, last):
-            nc.scalar.copy(y_all[:, first * C:last * C], ys[first][:].rearrange("p e c -> p (e c)"))
+        ys = {}
 
-        def put_back(a, b):
-            nc.vector.tensor_tensor(
-                window[:].indirect(offsets[:, a // 16:b // 16]), y_all[:, a:b], gates[:, a:b], MULT
+        def second_layer(e):
+            copy = nc.scalar.copy if e == LAST else nc.vector.tensor_copy
+            copy(
+                out=second[e][:, 1, :].rearrange("p (c i j) -> p c j i", i=4, j=PACK),
+                in_=w2_raw[:, e, :].rearrange("p (j c i) -> p c j i", i=4, j=PACK),
+            )
+            codes = work.tile([P, 2, C], U32, name=f"codes{e}", tag="codes", align_bytes=64)
+            scales = work.tile([P, 2, C], U8, name=f"scales{e}", tag="scales", align_bytes=64)
+            for part in (slice(1, 2), slice(0, 1)) if e == LAST else (slice(0, 2),):
+                nc.vector.quantize_mx(
+                    out=codes[:, part, :].rearrange("p a c -> p (a c)").bitcast(FP8X4),
+                    scales=scales[:, part, :].rearrange("p a c -> p (a c)"),
+                    in_=second[e][:, part, :].rearrange("p a f -> p (a f)"),
+                )
+            ys[e] = psum.tile([P, C], F32, name=f"y{e}", tag=f"y{e % 2}")
+            nc.tensor.matmul_mx(
+                out=ys[e][:],
+                lhsT=codes[:, 1, :].bitcast(FP8X4),
+                lhsT_scale=scales[:, 1, :],
+                rhs=codes[:, 0, :].bitcast(FP8X4),
+                rhs_scale=scales[:, 0, :],
+                start=True,
+                stop=True,
             )
 
-        gather(0)
-        group_tokens(0)
-        quantize_tokens(0)
-        gather(1)
-        group_tokens(1)
-        quantize_tokens(1)
-        gather(2)
-        group_tokens(2)
-        quantize_tokens(2)
-        group_w2(0, 2)
-        quantize_w2(0, 2)
-        group_w1(0, 48, False)
-        quantize_w1(0, False)
-        multiply_w1(0)
-        group_w1(1, 64, False)
-        quantize_w1(1, False)
-        multiply_w1(1)
-        group_w1(2, 96, False)
-        quantize_w1(2, False)
-        multiply_w1(2)
-        group_w1(3, 0, False)
-        quantize_w1(3, False)
-        multiply_w1(3)
-        group_w1(4, 64, False)
-        quantize_w1(4, False)
-        multiply_w1(4)
-        hidden_in(None, 0)
-        apply_gelu(0)
-        group_w1(5, 96, False)
-        quantize_w1(5, False)
-        multiply_w1(5)
-        group_w1(6, 0, False)
-        quantize_w1(6, False)
-        multiply_w1(6)
-        group_w1(7, 64, False)
-        quantize_w1(7, False)
-        multiply_w1(7)
-        apply_gelu(1)
-        multiply_w2(0, 2)
-        take_out(0, 2)
-        group_w1(8, 96, False)
-        quantize_w1(8, False)
-        multiply_w1(8)
-        put_back(0, 256)
-        group_w1(9, 0, False)
-        quantize_w1(9, False)
-        multiply_w1(9)
-        group_w1(10, 64, False)
-        quantize_w1(10, False)
-        multiply_w1(10)
-        hidden_in(None, 1)
-        apply_gelu(2)
-        group_w1(11, 56, False)
-        quantize_w1(11, False)
-        multiply_w1(11)
-        group_w2(2, 4)
-        quantize_w2(2, 4)
-        apply_gelu(3)
-        multiply_w2(2, 4)
-        take_out(2, 4)
-        put_back(256, 512)
+        def put_back(e):
+            gated = work.tile([P, C], F32, name=f"gated{e}", tag="gated")
+            nc.vector.tensor_tensor(gated[:], ys[e][:], gates[:, e * C:(e + 1) * C], MULT)
+            nc.vector.tensor_tensor(
+                window[:].indirect(offsets[:, e * C // 16:(e + 1) * C // 16]), gated[:], zeros[:], ADD
+            )
+
+        for s in range(PASSES):
+            prepare_tokens(s)
+        for e in range(E):
+            first_layer(e, 0)
+            if e > 0:
+                second_layer(e - 1)
+            first_layer(e, 1)
+            if e > 0:
+                put_back(e - 1)
+            first_layer(e, 2)
+            apply_gelu(e)
+        second_layer(LAST)
+        put_back(LAST)
         nc.sync.dma_start(out=out, in_=window[:])

@@ -10,8 +10,8 @@ K_PASS = P * PACK
 PASSES = K // K_PASS
 FLOPS = 2 * SLOTS * (K * H + H * N)
 LAST = E - 1
-SCALAR_SHARE = (0, 84, 64)
-SCALAR_SHARE_LAST = 88
+SCALAR_SHARE = (0, 96, 80)
+LAST_SHARES = (36, 84)
 RAW_BUFS = 12
 
 F32 = mybir.dt.float32
@@ -61,14 +61,15 @@ def tile_routed_moe_kernel(tc, xT, w1, w2, gate, offs, out):
             load_x(s)
         for e in range(E):
             load_w1(e, 0)
-            if e > 0:
+            if 0 < e < LAST:
                 load_w2(e - 1)
             load_w1(e, 1)
-            if e > 0:
+            if 0 < e < LAST:
                 load_gate((e - 1) * C, e * C)
             load_w1(e, 2)
+        load_w2(LAST - 1)
         load_w2(LAST)
-        load_gate(LAST * C, SLOTS)
+        load_gate((LAST - 1) * C, SLOTS)
 
         window = keep.tile([P, T], F32, name="window")
         nc.gpsimd.memset(window[:], 0.0)
@@ -132,14 +133,14 @@ def tile_routed_moe_kernel(tc, xT, w1, w2, gate, offs, out):
                     scales = work.tile([P, PASSES, H], U8, name=f"w1_scales{e}", tag="w1_scales", align_bytes=64)
                     w1_codes[e], w1_scales[e] = codes[:], scales[:]
             if (e, s) == (LAST, PASSES - 1):
-                cut = SCALAR_SHARE_LAST
-                copy_w1(nc.vector.tensor_copy, e, s, slice(0, P), slice(0, 2))
-                copy_w1(nc.scalar.copy, e, s, slice(0, cut), slice(2, 4))
-                copy_w1(nc.vector.tensor_copy, e, s, slice(cut, P), slice(2, 4))
-                quantize_w1(e, s, 0, H // 2)
-                quantize_w1(e, s, H // 2, H)
+                for t, cut in ((slice(0, 2), LAST_SHARES[0]), (slice(2, 4), LAST_SHARES[1])):
+                    copy_w1(nc.scalar.copy, e, s, slice(0, cut), t)
+                    copy_w1(nc.vector.tensor_copy, e, s, slice(cut, P), t)
+                quantize_w1(e, s, 0, P)
+                quantize_w1(e, s, P, 2 * P)
+                quantize_w1(e, s, 2 * P, H)
             else:
-                cut = SCALAR_SHARE[s]
+                cut = 52 if (e, s) == (LAST, 1) else SCALAR_SHARE[s]
                 copy_w1(nc.scalar.copy, e, s, slice(0, cut), slice(0, 4))
                 copy_w1(nc.vector.tensor_copy, e, s, slice(cut, P), slice(0, 4))
                 if e == 0:
@@ -172,7 +173,7 @@ def tile_routed_moe_kernel(tc, xT, w1, w2, gate, offs, out):
         ys = {}
 
         def second_layer(e):
-            copy = nc.scalar.copy if e == LAST else nc.vector.tensor_copy
+            copy = nc.scalar.copy if e == LAST - 1 else nc.vector.tensor_copy
             copy(
                 out=second[e][:, 1, :].rearrange("p (c i j) -> p c j i", i=4, j=PACK),
                 in_=w2_raw[:, e, :].rearrange("p (j c i) -> p c j i", i=4, j=PACK),
@@ -207,12 +208,15 @@ def tile_routed_moe_kernel(tc, xT, w1, w2, gate, offs, out):
             prepare_tokens(s)
         for e in range(E):
             first_layer(e, 0)
-            if e > 0:
+            if 0 < e < LAST:
                 second_layer(e - 1)
             first_layer(e, 1)
-            if e > 0:
+            if 0 < e < LAST:
                 put_back(e - 1)
             first_layer(e, 2)
+            if e == LAST:
+                second_layer(e - 1)
+                put_back(e - 1)
             apply_gelu(e)
         second_layer(LAST)
         put_back(LAST)

@@ -12,7 +12,7 @@ FLOPS = 2 * SLOTS * (K * H + H * N)
 LAST = E - 1
 SCALAR_SHARE = (0, 96, 80)
 LAST_SHARES = (36, 84)
-RAW_BUFS = 12
+RAW_BUFS = 9
 
 F32 = mybir.dt.float32
 BF16 = mybir.dt.bfloat16
@@ -34,20 +34,21 @@ def tile_routed_moe_kernel(tc, xT, w1, w2, gate, offs, out):
         psum = ctx.enter_context(tc.psum_pool(name="psum", bufs=1))
 
         offsets = keep.tile([P, SLOTS // 16], U16, name="offsets")
-        nc.sync.dma_start(offsets[:], offs)
 
         x_raw, w1_raw = {}, {}
         w2_raw = keep.tile([P, E, PACK * N], F32, name="w2_raw")
         gates = keep.tile([P, SLOTS], F32, name="gates")
 
-        def load_x(s):
-            rows = xT[s * K_PASS:(s + 1) * K_PASS, :].rearrange("(p j) n -> p j n", j=PACK)
-            for j in range(PACK):
-                x_raw[s, j] = raws.tile([P, T], F32, name=f"x_raw{s}{j}", tag="raw", bufs=RAW_BUFS)
-                nc.sync.dma_start(out=x_raw[s, j][:], in_=rows[:, j, :])
+        def load_x(s, planes):
+            rows = xT[s * K_PASS:(s + 1) * K_PASS, :].rearrange("(p j) n -> p (j n)", j=PACK)
+            for j in range(0, PACK, planes):
+                raw = raws.tile([P, planes * T], F32, name=f"x_raw{s}{j}", tag=f"raw{planes}", bufs=RAW_BUFS if planes == 1 else PACK // planes)
+                nc.sync.dma_start(out=raw[:], in_=rows[:, j * T:(j + planes) * T])
+                for i in range(planes):
+                    x_raw[s, j + i] = raw[:, i * T:(i + 1) * T]
 
         def load_w1(e, s):
-            w1_raw[e, s] = raws.tile([P, PACK * H], F32, name=f"w1_raw{e}{s}", tag="raw", bufs=RAW_BUFS)
+            w1_raw[e, s] = raws.tile([P, PACK * H], F32, name=f"w1_raw{e}{s}", tag="raw1", bufs=RAW_BUFS)
             rows = w1[e, s * K_PASS:(s + 1) * K_PASS, :].rearrange("(p j) c -> p (j c)", j=PACK)
             nc.sync.dma_start(out=w1_raw[e, s][:], in_=rows)
 
@@ -58,7 +59,9 @@ def tile_routed_moe_kernel(tc, xT, w1, w2, gate, offs, out):
             nc.sync.dma_start(out=gates[:, a:b], in_=gate[:, a:b])
 
         for s in range(PASSES):
-            load_x(s)
+            load_x(s, PACK >> s)
+            if s == 0:
+                nc.sync.dma_start(offsets[:], offs)
         for e in range(E):
             load_w1(e, 0)
             if 0 < e < LAST:
@@ -87,7 +90,7 @@ def tile_routed_moe_kernel(tc, xT, w1, w2, gate, offs, out):
         def prepare_tokens(s):
             picked = work.tile([P, PACK, SLOTS], F32, name=f"picked{s}", tag="picked")
             for j in range(PACK):
-                nc.vector.tensor_copy(picked[:, j, :], x_raw[s, j][:].indirect(offsets[:]))
+                nc.vector.tensor_copy(picked[:, j, :], x_raw[s, j].indirect(offsets[:]))
             nc.scalar.copy(
                 out=first_grouped[:, s, 0, :].rearrange("p (c i j) -> p c j i", i=4, j=PACK),
                 in_=picked[:].rearrange("p j (c i) -> p c j i", i=4),

@@ -12,7 +12,7 @@ FLOPS = 2 * SLOTS * (K * H + H * N)
 LAST = E - 1
 SCALAR_SHARE = (0, 96, 80)
 LAST_SHARES = (36, 84)
-RAW_BUFS = 9
+RAW_BUFS = 6
 
 F32 = mybir.dt.float32
 BF16 = mybir.dt.bfloat16
@@ -41,11 +41,12 @@ def tile_routed_moe_kernel(tc, xT, w1, w2, gate, offs, out):
 
         def load_x(s, planes):
             rows = xT[s * K_PASS:(s + 1) * K_PASS, :].rearrange("(p j) n -> p (j n)", j=PACK)
+            raw = keep.tile([P, PACK * T], F32, name=f"x_raw{s}")
             for j in range(0, PACK, planes):
-                raw = raws.tile([P, planes * T], F32, name=f"x_raw{s}{j}", tag=f"raw{planes}", bufs=RAW_BUFS if planes == 1 else PACK // planes)
-                nc.sync.dma_start(out=raw[:], in_=rows[:, j * T:(j + planes) * T])
-                for i in range(planes):
-                    x_raw[s, j + i] = raw[:, i * T:(i + 1) * T]
+                cols = slice(j * T, (j + planes) * T)
+                nc.sync.dma_start(out=raw[:, cols], in_=rows[:, cols])
+            for j in range(PACK):
+                x_raw[s, j] = raw[:, j * T:(j + 1) * T]
 
         def load_w1(e, s):
             w1_raw[e, s] = raws.tile([P, PACK * H], F32, name=f"w1_raw{e}{s}", tag="raw1", bufs=RAW_BUFS)
@@ -59,7 +60,7 @@ def tile_routed_moe_kernel(tc, xT, w1, w2, gate, offs, out):
             nc.sync.dma_start(out=gates[:, a:b], in_=gate[:, a:b])
 
         for s in range(PASSES):
-            load_x(s, PACK >> s)
+            load_x(s, 2 if s == PASSES - 1 else PACK)
             if s == 0:
                 nc.sync.dma_start(offsets[:], offs)
         for e in range(E):
@@ -67,8 +68,8 @@ def tile_routed_moe_kernel(tc, xT, w1, w2, gate, offs, out):
             if 0 < e < LAST:
                 load_w2(e - 1)
             load_w1(e, 1)
-            if 0 < e < LAST:
-                load_gate((e - 1) * C, e * C)
+            if e == 1:
+                load_gate(0, 2 * C)
             load_w1(e, 2)
         load_w2(LAST - 1)
         load_w2(LAST)
@@ -143,7 +144,7 @@ def tile_routed_moe_kernel(tc, xT, w1, w2, gate, offs, out):
                 quantize_w1(e, s, P, 2 * P)
                 quantize_w1(e, s, 2 * P, H)
             else:
-                cut = 52 if (e, s) == (LAST, 1) else SCALAR_SHARE[s]
+                cut = 52 if s == 1 and e in (0, LAST) else SCALAR_SHARE[s]
                 copy_w1(nc.scalar.copy, e, s, slice(0, cut), slice(0, 4))
                 copy_w1(nc.vector.tensor_copy, e, s, slice(cut, P), slice(0, 4))
                 if e == 0:

@@ -10,9 +10,13 @@ K_PASS = P * PACK
 PASSES = K // K_PASS
 FLOPS = 2 * SLOTS * (K * H + H * N)
 LAST = E - 1
-SCALAR_SHARE = (0, 96, 80)
-LAST_SHARES = (36, 84)
-RAW_BUFS = 6
+LIST_ROWS = 16
+
+SCALAR_GROUPS = (0, 96, 80)
+SCALAR_GROUPS_NO_SECOND_LAYER = 52
+SCALAR_GROUPS_LAST_PASS = (44, 76)
+W1_RAW_BUFS = 6
+W1_GROUPED_BUFS = 4
 
 F32 = mybir.dt.float32
 BF16 = mybir.dt.bfloat16
@@ -33,34 +37,31 @@ def tile_routed_moe_kernel(tc, xT, w1, w2, gate, offs, out):
         work = ctx.enter_context(tc.tile_pool(name="work", bufs=2))
         psum = ctx.enter_context(tc.psum_pool(name="psum", bufs=1))
 
-        offsets = keep.tile([P, SLOTS // 16], U16, name="offsets")
-
+        offsets = keep.tile([P, SLOTS // LIST_ROWS], U16, name="offsets")
         x_raw, w1_raw = {}, {}
         w2_raw = keep.tile([P, E, PACK * N], F32, name="w2_raw")
         gates = keep.tile([P, SLOTS], F32, name="gates")
 
-        def load_x(s, planes):
+        def load_x(s, rows_per_load):
             rows = xT[s * K_PASS:(s + 1) * K_PASS, :].rearrange("(p j) n -> p (j n)", j=PACK)
-            raw = keep.tile([P, PACK * T], F32, name=f"x_raw{s}")
-            for j in range(0, PACK, planes):
-                cols = slice(j * T, (j + planes) * T)
-                nc.sync.dma_start(out=raw[:, cols], in_=rows[:, cols])
-            for j in range(PACK):
-                x_raw[s, j] = raw[:, j * T:(j + 1) * T]
+            x_raw[s] = keep.tile([P, PACK * T], F32, name=f"x_raw{s}")
+            for j in range(0, PACK, rows_per_load):
+                cols = slice(j * T, (j + rows_per_load) * T)
+                nc.sync.dma_start(out=x_raw[s][:, cols], in_=rows[:, cols])
 
         def load_w1(e, s):
-            w1_raw[e, s] = raws.tile([P, PACK * H], F32, name=f"w1_raw{e}{s}", tag="raw1", bufs=RAW_BUFS)
+            w1_raw[e, s] = raws.tile([P, PACK * H], F32, name=f"w1_raw{e}{s}", tag="w1_raw", bufs=W1_RAW_BUFS)
             rows = w1[e, s * K_PASS:(s + 1) * K_PASS, :].rearrange("(p j) c -> p (j c)", j=PACK)
             nc.sync.dma_start(out=w1_raw[e, s][:], in_=rows)
 
         def load_w2(e):
             nc.sync.dma_start(out=w2_raw[:, e, :], in_=w2[e].rearrange("(p j) n -> p (j n)", j=PACK))
 
-        def load_gate(a, b):
-            nc.sync.dma_start(out=gates[:, a:b], in_=gate[:, a:b])
+        def load_gate(first, end):
+            nc.sync.dma_start(out=gates[:, first * C:end * C], in_=gate[:, first * C:end * C])
 
         for s in range(PASSES):
-            load_x(s, 2 if s == PASSES - 1 else PACK)
+            load_x(s, PACK // 2 if s == PASSES - 1 else PACK)
             if s == 0:
                 nc.sync.dma_start(offsets[:], offs)
         for e in range(E):
@@ -69,51 +70,51 @@ def tile_routed_moe_kernel(tc, xT, w1, w2, gate, offs, out):
                 load_w2(e - 1)
             load_w1(e, 1)
             if e == 1:
-                load_gate(0, 2 * C)
+                load_gate(0, LAST - 1)
             load_w1(e, 2)
         load_w2(LAST - 1)
         load_w2(LAST)
-        load_gate((LAST - 1) * C, SLOTS)
+        load_gate(LAST - 1, E)
 
         window = keep.tile([P, T], F32, name="window")
         nc.gpsimd.memset(window[:], 0.0)
         zeros = keep.tile([P, C], F32, name="zeros")
         nc.gpsimd.memset(zeros[:], 0.0)
-        warm = keep.tile([P, 1], F32, name="warm")
-        nc.gpsimd.memset(warm[:], 0.0)
-        nc.scalar.activation(warm[:], warm[:], GELU)
 
         first_grouped = keep.tile([P, PASSES, 2, SLOTS * PACK], BF16, name="first_grouped", align_bytes=64)
         first_codes = keep.tile([P, PASSES, 2, SLOTS], U32, name="first_codes", align_bytes=64)
         first_scales = keep.tile([P, PASSES, 2, SLOTS], U8, name="first_scales", align_bytes=64)
         x_codes, x_scales = first_codes[:, :, 0, :], first_scales[:, :, 0, :]
 
-        def prepare_tokens(s):
+        def quantize(codes, scales, grouped):
+            nc.vector.quantize_mx(out=codes.bitcast(FP8X4), scales=scales, in_=grouped)
+
+        def merged(ap):
+            return ap.rearrange("p a f -> p (a f)")
+
+        def interleave(copy, grouped, raw):
+            copy(
+                out=grouped.rearrange("p (c i j) -> p c j i", i=4, j=PACK),
+                in_=raw.rearrange("p (j c i) -> p c j i", i=4, j=PACK),
+            )
+
+        def gather_tokens(s):
             picked = work.tile([P, PACK, SLOTS], F32, name=f"picked{s}", tag="picked")
             for j in range(PACK):
-                nc.vector.tensor_copy(picked[:, j, :], x_raw[s, j].indirect(offsets[:]))
-            nc.scalar.copy(
-                out=first_grouped[:, s, 0, :].rearrange("p (c i j) -> p c j i", i=4, j=PACK),
-                in_=picked[:].rearrange("p j (c i) -> p c j i", i=4),
-            )
+                nc.vector.tensor_copy(picked[:, j, :], x_raw[s][:, j * T:(j + 1) * T].indirect(offsets[:]))
+            interleave(nc.scalar.copy, first_grouped[:, s, 0, :], merged(picked[:]))
 
-        w1_codes, w1_scales, w1_grouped, sums = {}, {}, {}, {}
+        w1_codes, w1_scales, sums = {}, {}, {}
 
-        def copy_w1(copy, e, s, m, t):
-            if m.start < m.stop:
-                copy(
-                    out=w1_grouped[e, s].rearrange("p (t m j) -> p m j t", t=4, j=PACK)[:, m, :, t],
-                    in_=w1_raw[e, s][:].rearrange("p (j m t) -> p m j t", j=PACK, t=4)[:, m, :, t],
-                )
+        def interleave_w1(grouped, raw, scalar_groups, t):
+            for copy, m in ((nc.scalar.copy, slice(0, scalar_groups)), (nc.vector.tensor_copy, slice(scalar_groups, P))):
+                if m.start < m.stop:
+                    copy(
+                        out=grouped.rearrange("p (t m j) -> p m j t", t=4, j=PACK)[:, m, :, t],
+                        in_=raw.rearrange("p (j m t) -> p m j t", j=PACK, t=4)[:, m, :, t],
+                    )
 
-        def quantize_w1(e, s, a, b):
-            nc.vector.quantize_mx(
-                out=w1_codes[e][:, s, a:b].bitcast(FP8X4),
-                scales=w1_scales[e][:, s, a:b],
-                in_=w1_grouped[e, s][:, a * PACK:b * PACK],
-            )
-
-        def pass_w1(e, s, t):
+        def multiply_w1(e, s, t):
             cols, slots = slice(t * P, (t + 1) * P), slice(e * C, (e + 1) * C)
             nc.tensor.matmul_mx(
                 out=sums[e, t // 2][:, t % 2, :],
@@ -126,70 +127,60 @@ def tile_routed_moe_kernel(tc, xT, w1, w2, gate, offs, out):
             )
 
         def first_layer(e, s):
+            raw = w1_raw[e, s][:]
             if e == 0:
-                w1_grouped[e, s] = first_grouped[:, s, 1, :]
+                grouped = first_grouped[:, s, 1, :]
                 w1_codes[e], w1_scales[e] = first_codes[:, :, 1, :], first_scales[:, :, 1, :]
             else:
-                grouped = work.tile([P, H * PACK], BF16, name=f"w1_grouped{e}{s}", tag="w1_grouped", align_bytes=64, bufs=4)
-                w1_grouped[e, s] = grouped[:]
+                grouped = work.tile(
+                    [P, H * PACK], BF16, name=f"w1_grouped{e}{s}", tag="w1_grouped", align_bytes=64, bufs=W1_GROUPED_BUFS
+                )
+                grouped = grouped[:]
                 if s == 0:
                     codes = work.tile([P, PASSES, H], U32, name=f"w1_codes{e}", tag="w1_codes", align_bytes=64)
                     scales = work.tile([P, PASSES, H], U8, name=f"w1_scales{e}", tag="w1_scales", align_bytes=64)
                     w1_codes[e], w1_scales[e] = codes[:], scales[:]
             if (e, s) == (LAST, PASSES - 1):
-                for t, cut in ((slice(0, 2), LAST_SHARES[0]), (slice(2, 4), LAST_SHARES[1])):
-                    copy_w1(nc.scalar.copy, e, s, slice(0, cut), t)
-                    copy_w1(nc.vector.tensor_copy, e, s, slice(cut, P), t)
-                quantize_w1(e, s, 0, P)
-                quantize_w1(e, s, P, 2 * P)
-                quantize_w1(e, s, 2 * P, H)
+                for half, scalar_groups in enumerate(SCALAR_GROUPS_LAST_PASS):
+                    interleave_w1(grouped, raw, scalar_groups, slice(2 * half, 2 * half + 2))
+                for t in range(4):
+                    cols = slice(t * P, (t + 1) * P)
+                    quantize(w1_codes[e][:, s, cols], w1_scales[e][:, s, cols], grouped[:, t * K_PASS:(t + 1) * K_PASS])
             else:
-                cut = 52 if s == 1 and e in (0, LAST) else SCALAR_SHARE[s]
-                copy_w1(nc.scalar.copy, e, s, slice(0, cut), slice(0, 4))
-                copy_w1(nc.vector.tensor_copy, e, s, slice(cut, P), slice(0, 4))
+                scalar_groups = SCALAR_GROUPS_NO_SECOND_LAYER if s == 1 and e in (0, LAST) else SCALAR_GROUPS[s]
+                interleave_w1(grouped, raw, scalar_groups, slice(0, 4))
                 if e == 0:
-                    nc.vector.quantize_mx(
-                        out=first_codes[:, s].rearrange("p a c -> p (a c)").bitcast(FP8X4),
-                        scales=first_scales[:, s].rearrange("p a c -> p (a c)"),
-                        in_=first_grouped[:, s].rearrange("p a f -> p (a f)"),
-                    )
+                    quantize(merged(first_codes[:, s]), merged(first_scales[:, s]), merged(first_grouped[:, s]))
                 else:
-                    quantize_w1(e, s, 0, H)
+                    quantize(w1_codes[e][:, s, :], w1_scales[e][:, s, :], grouped)
             for q in range(2):
                 if s == 0:
-                    sums[e, q] = psum.tile([P, 2, C], F32, name=f"acc{e}{q}", tag=f"acc{e % 2}{q}")
-                pass_w1(e, s, 2 * q)
+                    sums[e, q] = psum.tile([P, 2, C], F32, name=f"sums{e}{q}", tag=f"sums{e % 2}{q}")
+                multiply_w1(e, s, 2 * q)
                 if s == PASSES - 1:
                     for r in range(PASSES):
-                        pass_w1(e, r, 2 * q + 1)
+                        multiply_w1(e, r, 2 * q + 1)
 
-        second = {}
+        second_grouped, ys = {}, {}
 
         def apply_gelu(e):
-            second[e] = work.tile([P, 2, C * PACK], BF16, name=f"second{e}", tag="second", align_bytes=64)
+            second_grouped[e] = work.tile(
+                [P, 2, C * PACK], BF16, name=f"second_grouped{e}", tag="second_grouped", align_bytes=64
+            )
             for q in range(2):
                 nc.scalar.activation(
-                    second[e][:, 0, :].rearrange("p (n q t) -> p q n t", q=2, t=2)[:, q],
+                    second_grouped[e][:, 0, :].rearrange("p (n q t) -> p q n t", q=2, t=2)[:, q],
                     sums[e, q][:].rearrange("p t n -> p n t"),
                     GELU,
                 )
 
-        ys = {}
-
         def second_layer(e):
             copy = nc.scalar.copy if e == LAST - 1 else nc.vector.tensor_copy
-            copy(
-                out=second[e][:, 1, :].rearrange("p (c i j) -> p c j i", i=4, j=PACK),
-                in_=w2_raw[:, e, :].rearrange("p (j c i) -> p c j i", i=4, j=PACK),
-            )
-            codes = work.tile([P, 2, C], U32, name=f"codes{e}", tag="codes", align_bytes=64)
-            scales = work.tile([P, 2, C], U8, name=f"scales{e}", tag="scales", align_bytes=64)
+            interleave(copy, second_grouped[e][:, 1, :], w2_raw[:, e, :])
+            codes = work.tile([P, 2, C], U32, name=f"second_codes{e}", tag="second_codes", align_bytes=64)
+            scales = work.tile([P, 2, C], U8, name=f"second_scales{e}", tag="second_scales", align_bytes=64)
             for part in (slice(1, 2), slice(0, 1)) if e == LAST else (slice(0, 2),):
-                nc.vector.quantize_mx(
-                    out=codes[:, part, :].rearrange("p a c -> p (a c)").bitcast(FP8X4),
-                    scales=scales[:, part, :].rearrange("p a c -> p (a c)"),
-                    in_=second[e][:, part, :].rearrange("p a f -> p (a f)"),
-                )
+                quantize(merged(codes[:, part, :]), merged(scales[:, part, :]), merged(second_grouped[e][:, part, :]))
             ys[e] = psum.tile([P, C], F32, name=f"y{e}", tag=f"y{e % 2}")
             nc.tensor.matmul_mx(
                 out=ys[e][:],
@@ -204,12 +195,11 @@ def tile_routed_moe_kernel(tc, xT, w1, w2, gate, offs, out):
         def put_back(e):
             gated = work.tile([P, C], F32, name=f"gated{e}", tag="gated")
             nc.vector.tensor_tensor(gated[:], ys[e][:], gates[:, e * C:(e + 1) * C], MULT)
-            nc.vector.tensor_tensor(
-                window[:].indirect(offsets[:, e * C // 16:(e + 1) * C // 16]), gated[:], zeros[:], ADD
-            )
+            entries = slice(e * C // LIST_ROWS, (e + 1) * C // LIST_ROWS)
+            nc.vector.tensor_tensor(window[:].indirect(offsets[:, entries]), gated[:], zeros[:], ADD)
 
         for s in range(PASSES):
-            prepare_tokens(s)
+            gather_tokens(s)
         for e in range(E):
             first_layer(e, 0)
             if 0 < e < LAST:

@@ -12,9 +12,9 @@ FLOPS = 2 * SLOTS * (K * H + H * N)
 LAST = E - 1
 LIST_ROWS = 16
 
-SCALAR_GROUPS = (0, 96, 80)
+SCALAR_GROUPS = (56, 96, 80)
 SCALAR_GROUPS_NO_SECOND_LAYER = 52
-SCALAR_GROUPS_LAST_PASS = (44, 76)
+SCALAR_GROUPS_LAST_PASS = (56, 24)
 W1_RAW_BUFS = 6
 W1_GROUPED_BUFS = 4
 
@@ -114,16 +114,19 @@ def tile_routed_moe_kernel(tc, xT, w1, w2, gate, offs, out):
                         in_=raw.rearrange("p (j m t) -> p m j t", j=PACK, t=4)[:, m, :, t],
                     )
 
+        def per_bank(e):
+            return 2 if e == LAST else 4
+
         def multiply_w1(e, s, t):
             cols, slots = slice(t * P, (t + 1) * P), slice(e * C, (e + 1) * C)
             nc.tensor.matmul_mx(
-                out=sums[e, t // 2][:, t % 2, :],
+                out=sums[e, t // per_bank(e)][:, t % per_bank(e), :],
                 lhsT=w1_codes[e][:, s, cols].bitcast(FP8X4),
                 lhsT_scale=w1_scales[e][:, s, cols],
                 rhs=x_codes[:, s, slots].bitcast(FP8X4),
                 rhs_scale=x_scales[:, s, slots],
-                start=(s == 0),
-                stop=(s == PASSES - 1),
+                start=(s == 0 and t % per_bank(e) == 0),
+                stop=(s == PASSES - 1 and t % per_bank(e) == per_bank(e) - 1),
             )
 
         def first_layer(e, s):
@@ -148,18 +151,18 @@ def tile_routed_moe_kernel(tc, xT, w1, w2, gate, offs, out):
                     quantize(w1_codes[e][:, s, cols], w1_scales[e][:, s, cols], grouped[:, t * K_PASS:(t + 1) * K_PASS])
             else:
                 scalar_groups = SCALAR_GROUPS_NO_SECOND_LAYER if s == 1 and e in (0, LAST) else SCALAR_GROUPS[s]
+                if (e, s) == (0, 0):
+                    scalar_groups = 0
                 interleave_w1(grouped, raw, scalar_groups, slice(0, 4))
                 if e == 0:
                     quantize(merged(first_codes[:, s]), merged(first_scales[:, s]), merged(first_grouped[:, s]))
                 else:
                     quantize(w1_codes[e][:, s, :], w1_scales[e][:, s, :], grouped)
-            for q in range(2):
-                if s == 0:
-                    sums[e, q] = psum.tile([P, 2, C], F32, name=f"sums{e}{q}", tag=f"sums{e % 2}{q}")
-                multiply_w1(e, s, 2 * q)
-                if s == PASSES - 1:
-                    for r in range(PASSES):
-                        multiply_w1(e, r, 2 * q + 1)
+            for t in range(4):
+                if s == 0 and t % per_bank(e) == 0:
+                    q = t // per_bank(e)
+                    sums[e, q] = psum.tile([P, per_bank(e), C], F32, name=f"sums{e}{q}", tag=f"sums{e}{q}")
+                multiply_w1(e, s, t)
 
         second_grouped, ys = {}, {}
 
@@ -167,15 +170,15 @@ def tile_routed_moe_kernel(tc, xT, w1, w2, gate, offs, out):
             second_grouped[e] = work.tile(
                 [P, 2, C * PACK], BF16, name=f"second_grouped{e}", tag="second_grouped", align_bytes=64
             )
-            for q in range(2):
+            for q in range(4 // per_bank(e)):
                 nc.scalar.activation(
-                    second_grouped[e][:, 0, :].rearrange("p (n q t) -> p q n t", q=2, t=2)[:, q],
+                    second_grouped[e][:, 0, :].rearrange("p (n q t) -> p q n t", n=C, t=per_bank(e))[:, q],
                     sums[e, q][:].rearrange("p t n -> p n t"),
                     GELU,
                 )
 
         def second_layer(e):
-            copy = nc.scalar.copy if e == LAST - 1 else nc.vector.tensor_copy
+            copy = nc.scalar.copy if e >= LAST - 1 else nc.vector.tensor_copy
             interleave(copy, second_grouped[e][:, 1, :], w2_raw[:, e, :])
             codes = work.tile([P, 2, C], U32, name=f"second_codes{e}", tag="second_codes", align_bytes=64)
             scales = work.tile([P, 2, C], U8, name=f"second_scales{e}", tag="second_scales", align_bytes=64)

@@ -79,7 +79,7 @@ def tile_routed_moe_kernel(tc, xT, w1, w2, gate, offs, out):
         window = keep.tile([P, T], F32, name="window")
         nc.gpsimd.memset(window[:], 0.0)
         zeros = keep.tile([P, C], F32, name="zeros")
-        nc.gpsimd.memset(zeros[:], 0.0)
+        nc.scalar.activation(zeros[:], window[:, 0:C], GELU)
 
         first_grouped = keep.tile([P, PASSES, 2, SLOTS * PACK], BF16, name="first_grouped", align_bytes=64)
         first_codes = keep.tile([P, PASSES, 2, SLOTS], U32, name="first_codes", align_bytes=64)

@@ -13,6 +13,7 @@ LAST = E - 1
 LIST_ROWS = 16
 
 SCALAR_GROUPS = (56, 96, 80)
+SCALAR_GROUPS_FIRST_EXPERT = (P, 0, SCALAR_GROUPS[2])
 SCALAR_GROUPS_NO_SECOND_LAYER = 52
 SCALAR_GROUPS_LAST_PASS = (56, 24)
 W1_RAW_BUFS = 6
@@ -33,7 +34,7 @@ def tile_routed_moe_kernel(tc, xT, w1, w2, gate, offs, out):
     nc = tc.nc
     with ExitStack() as ctx:
         keep = ctx.enter_context(tc.tile_pool(name="keep", bufs=1))
-        raws = ctx.enter_context(tc.tile_pool(name="raws", bufs=2))
+        raws = ctx.enter_context(tc.tile_pool(name="raws", bufs=W1_RAW_BUFS))
         work = ctx.enter_context(tc.tile_pool(name="work", bufs=2))
         psum = ctx.enter_context(tc.psum_pool(name="psum", bufs=1))
 
@@ -42,15 +43,13 @@ def tile_routed_moe_kernel(tc, xT, w1, w2, gate, offs, out):
         w2_raw = keep.tile([P, E, PACK * N], F32, name="w2_raw")
         gates = keep.tile([P, SLOTS], F32, name="gates")
 
-        def load_x(s, rows_per_load):
-            rows = xT[s * K_PASS:(s + 1) * K_PASS, :].rearrange("(p j) n -> p (j n)", j=PACK)
+        def load_x(s):
             x_raw[s] = keep.tile([P, PACK * T], F32, name=f"x_raw{s}")
-            for j in range(0, PACK, rows_per_load):
-                cols = slice(j * T, (j + rows_per_load) * T)
-                nc.sync.dma_start(out=x_raw[s][:, cols], in_=rows[:, cols])
+            rows = xT[s * K_PASS:(s + 1) * K_PASS, :].rearrange("(p j) n -> p (j n)", j=PACK)
+            nc.sync.dma_start(out=x_raw[s][:], in_=rows)
 
         def load_w1(e, s):
-            w1_raw[e, s] = raws.tile([P, PACK * H], F32, name=f"w1_raw{e}{s}", tag="w1_raw", bufs=W1_RAW_BUFS)
+            w1_raw[e, s] = raws.tile([P, PACK * H], F32, name=f"w1_raw{e}{s}", tag="w1_raw", align_bytes=64)
             rows = w1[e, s * K_PASS:(s + 1) * K_PASS, :].rearrange("(p j) c -> p (j c)", j=PACK)
             nc.sync.dma_start(out=w1_raw[e, s][:], in_=rows)
 
@@ -61,7 +60,7 @@ def tile_routed_moe_kernel(tc, xT, w1, w2, gate, offs, out):
             nc.sync.dma_start(out=gates[:, first * C:end * C], in_=gate[:, first * C:end * C])
 
         for s in range(PASSES):
-            load_x(s, PACK // 2 if s == PASSES - 1 else PACK)
+            load_x(s)
             if s == 0:
                 nc.sync.dma_start(offsets[:], offs)
         for e in range(E):
@@ -72,19 +71,25 @@ def tile_routed_moe_kernel(tc, xT, w1, w2, gate, offs, out):
             if e == 1:
                 load_gate(0, LAST - 1)
             load_w1(e, 2)
-        load_w2(LAST - 1)
-        load_w2(LAST)
-        load_gate(LAST - 1, E)
+        for e in (LAST - 1, LAST):
+            load_w2(e)
+        for e in (LAST - 1, LAST):
+            load_gate(e, e + 1)
 
         window = keep.tile([P, T], F32, name="window")
         nc.gpsimd.memset(window[:], 0.0)
         zeros = keep.tile([P, C], F32, name="zeros")
         nc.scalar.activation(zeros[:], window[:, 0:C], GELU)
 
-        first_grouped = keep.tile([P, PASSES, 2, SLOTS * PACK], BF16, name="first_grouped", align_bytes=64)
-        first_codes = keep.tile([P, PASSES, 2, SLOTS], U32, name="first_codes", align_bytes=64)
-        first_scales = keep.tile([P, PASSES, 2, SLOTS], U8, name="first_scales", align_bytes=64)
-        x_codes, x_scales = first_codes[:, :, 0, :], first_scales[:, :, 0, :]
+        piece_codes = keep.tile([P, 2 * PASSES, SLOTS], U32, name="piece_codes", align_bytes=64)
+        piece_scales = keep.tile([P, 2 * PASSES, SLOTS], U8, name="piece_scales", align_bytes=64)
+        early_pieces = 2 * PASSES - 2
+        early_grouped = keep.tile([P, early_pieces, SLOTS * PACK], BF16, name="early_grouped", align_bytes=64)
+        late_grouped = w1_raw[0, 0][:].bitcast(BF16).rearrange("p (a f) -> p a f", a=2)
+        x_piece, w_piece = (0, 1, 4), (2, 3, 5)
+
+        def grouped_piece(piece):
+            return early_grouped[:, piece, :] if piece < early_pieces else late_grouped[:, piece - early_pieces, :]
 
         def quantize(codes, scales, grouped):
             nc.vector.quantize_mx(out=codes.bitcast(FP8X4), scales=scales, in_=grouped)
@@ -92,19 +97,25 @@ def tile_routed_moe_kernel(tc, xT, w1, w2, gate, offs, out):
         def merged(ap):
             return ap.rearrange("p a f -> p (a f)")
 
+        def quantize_pieces(first, end):
+            grouped = early_grouped[:, first:end, :] if first < early_pieces else late_grouped
+            quantize(merged(piece_codes[:, first:end, :]), merged(piece_scales[:, first:end, :]), merged(grouped))
+
         def interleave(copy, grouped, raw):
             copy(
                 out=grouped.rearrange("p (c i j) -> p c j i", i=4, j=PACK),
                 in_=raw.rearrange("p (j c i) -> p c j i", i=4, j=PACK),
             )
 
-        def gather_tokens(s):
-            picked = work.tile([P, PACK, SLOTS], F32, name=f"picked{s}", tag="picked")
-            for j in range(PACK):
-                nc.vector.tensor_copy(picked[:, j, :], x_raw[s][:, j * T:(j + 1) * T].indirect(offsets[:]))
-            interleave(nc.scalar.copy, first_grouped[:, s, 0, :], merged(picked[:]))
+        picked = {}
 
-        w1_codes, w1_scales, sums = {}, {}, {}
+        def gather_tokens(s):
+            picked[s] = work.tile([P, PACK, SLOTS], F32, name=f"picked{s}", tag="picked")
+            for j in range(PACK):
+                nc.vector.tensor_copy(picked[s][:, j, :], x_raw[s][:, j * T:(j + 1) * T].indirect(offsets[:]))
+
+        def interleave_tokens(s):
+            interleave(nc.scalar.copy, grouped_piece(x_piece[s]), merged(picked[s][:]))
 
         def interleave_w1(grouped, raw, scalar_groups, t):
             for copy, m in ((nc.scalar.copy, slice(0, scalar_groups)), (nc.vector.tensor_copy, slice(scalar_groups, P))):
@@ -114,55 +125,56 @@ def tile_routed_moe_kernel(tc, xT, w1, w2, gate, offs, out):
                         in_=raw.rearrange("p (j m t) -> p m j t", j=PACK, t=4)[:, m, :, t],
                     )
 
+        w1_codes, w1_scales, sums = {}, {}, {}
+
         def per_bank(e):
             return 2 if e == LAST else 4
 
-        def multiply_w1(e, s, t):
-            cols, slots = slice(t * P, (t + 1) * P), slice(e * C, (e + 1) * C)
-            nc.tensor.matmul_mx(
-                out=sums[e, t // per_bank(e)][:, t % per_bank(e), :],
-                lhsT=w1_codes[e][:, s, cols].bitcast(FP8X4),
-                lhsT_scale=w1_scales[e][:, s, cols],
-                rhs=x_codes[:, s, slots].bitcast(FP8X4),
-                rhs_scale=x_scales[:, s, slots],
-                start=(s == 0 and t % per_bank(e) == 0),
-                stop=(s == PASSES - 1 and t % per_bank(e) == per_bank(e) - 1),
-            )
+        def multiply_w1(e, s, codes, scales):
+            slots = slice(e * C, (e + 1) * C)
+            for t in range(4):
+                bank, place = divmod(t, per_bank(e))
+                if s == 0 and place == 0:
+                    sums[e, bank] = psum.tile([P, per_bank(e), C], F32, name=f"sums{e}{bank}", tag=f"sums{e}{bank}")
+                cols = slice(t * P, (t + 1) * P)
+                nc.tensor.matmul_mx(
+                    out=sums[e, bank][:, place, :],
+                    lhsT=codes[:, cols].bitcast(FP8X4),
+                    lhsT_scale=scales[:, cols],
+                    rhs=piece_codes[:, x_piece[s], slots].bitcast(FP8X4),
+                    rhs_scale=piece_scales[:, x_piece[s], slots],
+                    start=(s == 0 and place == 0),
+                    stop=(s == PASSES - 1 and place == per_bank(e) - 1),
+                )
+
+        def first_expert_pass(s):
+            interleave_w1(grouped_piece(w_piece[s]), w1_raw[0, s][:], SCALAR_GROUPS_FIRST_EXPERT[s], slice(0, 4))
+            if s == 0:
+                interleave_tokens(PASSES - 1)
+            first_piece = w_piece[s] if s == 1 else w_piece[s] - 1
+            quantize_pieces(first_piece, w_piece[s] + 1)
+            multiply_w1(0, s, piece_codes[:, w_piece[s], :], piece_scales[:, w_piece[s], :])
 
         def first_layer(e, s):
             raw = w1_raw[e, s][:]
-            if e == 0:
-                grouped = first_grouped[:, s, 1, :]
-                w1_codes[e], w1_scales[e] = first_codes[:, :, 1, :], first_scales[:, :, 1, :]
-            else:
-                grouped = work.tile(
-                    [P, H * PACK], BF16, name=f"w1_grouped{e}{s}", tag="w1_grouped", align_bytes=64, bufs=W1_GROUPED_BUFS
-                )
-                grouped = grouped[:]
-                if s == 0:
-                    codes = work.tile([P, PASSES, H], U32, name=f"w1_codes{e}", tag="w1_codes", align_bytes=64)
-                    scales = work.tile([P, PASSES, H], U8, name=f"w1_scales{e}", tag="w1_scales", align_bytes=64)
-                    w1_codes[e], w1_scales[e] = codes[:], scales[:]
+            grouped = work.tile(
+                [P, H * PACK], BF16, name=f"w1_grouped{e}{s}", tag="w1_grouped", align_bytes=64, bufs=W1_GROUPED_BUFS
+            )
+            if s == 0:
+                w1_codes[e] = work.tile([P, PASSES, H], U32, name=f"w1_codes{e}", tag="w1_codes", align_bytes=64)
+                w1_scales[e] = work.tile([P, PASSES, H], U8, name=f"w1_scales{e}", tag="w1_scales", align_bytes=64)
+            codes, scales = w1_codes[e][:, s, :], w1_scales[e][:, s, :]
             if (e, s) == (LAST, PASSES - 1):
                 for half, scalar_groups in enumerate(SCALAR_GROUPS_LAST_PASS):
-                    interleave_w1(grouped, raw, scalar_groups, slice(2 * half, 2 * half + 2))
+                    interleave_w1(grouped[:], raw, scalar_groups, slice(2 * half, 2 * half + 2))
                 for t in range(4):
                     cols = slice(t * P, (t + 1) * P)
-                    quantize(w1_codes[e][:, s, cols], w1_scales[e][:, s, cols], grouped[:, t * K_PASS:(t + 1) * K_PASS])
+                    quantize(codes[:, cols], scales[:, cols], grouped[:, t * K_PASS:(t + 1) * K_PASS])
             else:
-                scalar_groups = SCALAR_GROUPS_NO_SECOND_LAYER if s == 1 and e in (0, LAST) else SCALAR_GROUPS[s]
-                if (e, s) == (0, 0):
-                    scalar_groups = 0
-                interleave_w1(grouped, raw, scalar_groups, slice(0, 4))
-                if e == 0:
-                    quantize(merged(first_codes[:, s]), merged(first_scales[:, s]), merged(first_grouped[:, s]))
-                else:
-                    quantize(w1_codes[e][:, s, :], w1_scales[e][:, s, :], grouped)
-            for t in range(4):
-                if s == 0 and t % per_bank(e) == 0:
-                    q = t // per_bank(e)
-                    sums[e, q] = psum.tile([P, per_bank(e), C], F32, name=f"sums{e}{q}", tag=f"sums{e}{q}")
-                multiply_w1(e, s, t)
+                scalar_groups = SCALAR_GROUPS_NO_SECOND_LAYER if (e, s) == (LAST, 1) else SCALAR_GROUPS[s]
+                interleave_w1(grouped[:], raw, scalar_groups, slice(0, 4))
+                quantize(codes, scales, grouped[:])
+            multiply_w1(e, s, codes, scales)
 
         second_grouped, ys = {}, {}
 
@@ -170,10 +182,10 @@ def tile_routed_moe_kernel(tc, xT, w1, w2, gate, offs, out):
             second_grouped[e] = work.tile(
                 [P, 2, C * PACK], BF16, name=f"second_grouped{e}", tag="second_grouped", align_bytes=64
             )
-            for q in range(4 // per_bank(e)):
+            for bank in range(4 // per_bank(e)):
                 nc.scalar.activation(
-                    second_grouped[e][:, 0, :].rearrange("p (n q t) -> p q n t", n=C, t=per_bank(e))[:, q],
-                    sums[e, q][:].rearrange("p t n -> p n t"),
+                    second_grouped[e][:, 0, :].rearrange("p (n q t) -> p q n t", n=C, t=per_bank(e))[:, bank],
+                    sums[e, bank][:].rearrange("p t n -> p n t"),
                     GELU,
                 )
 
@@ -196,19 +208,30 @@ def tile_routed_moe_kernel(tc, xT, w1, w2, gate, offs, out):
             )
 
         def put_back(e):
-            gated = work.tile([P, C], F32, name=f"gated{e}", tag="gated")
-            nc.vector.tensor_tensor(gated[:], ys[e][:], gates[:, e * C:(e + 1) * C], MULT)
+            if e == 1:
+                gated = w1_raw[e + 1, 1][:, PACK * H - C:]
+            else:
+                gated_tile = work.tile([P, C], F32, name=f"gated{e}", tag="gated")
+                gated = gated_tile[:]
+            nc.vector.tensor_tensor(gated, ys[e][:], gates[:, e * C:(e + 1) * C], MULT)
             entries = slice(e * C // LIST_ROWS, (e + 1) * C // LIST_ROWS)
-            nc.vector.tensor_tensor(window[:].indirect(offsets[:, entries]), gated[:], zeros[:], ADD)
+            nc.vector.tensor_tensor(window[:].indirect(offsets[:, entries]), gated, zeros[:], ADD)
 
         for s in range(PASSES):
             gather_tokens(s)
-        for e in range(E):
+            if s < PASSES - 1:
+                interleave_tokens(s)
+            if s == 0:
+                quantize_pieces(0, 1)
+        for s in range(PASSES):
+            first_expert_pass(s)
+        apply_gelu(0)
+        for e in range(1, E):
             first_layer(e, 0)
-            if 0 < e < LAST:
+            if e < LAST:
                 second_layer(e - 1)
             first_layer(e, 1)
-            if 0 < e < LAST:
+            if e < LAST:
                 put_back(e - 1)
             first_layer(e, 2)
             if e == LAST:

@@ -16,6 +16,7 @@ SCALAR_GROUPS = (56, 96, 80)
 SCALAR_GROUPS_FIRST_EXPERT = (P, 0, SCALAR_GROUPS[2])
 SCALAR_GROUPS_NO_SECOND_LAYER = 52
 SCALAR_GROUPS_LAST_PASS = (56, 24)
+DMA_ALIGN = 256
 W1_RAW_BUFS = 6
 W1_GROUPED_BUFS = 4
 
@@ -40,16 +41,18 @@ def tile_routed_moe_kernel(tc, xT, w1, w2, gate, offs, out):
 
         offsets = keep.tile([P, SLOTS // LIST_ROWS], U16, name="offsets")
         x_raw, w1_raw = {}, {}
-        w2_raw = keep.tile([P, E, PACK * N], F32, name="w2_raw")
-        gates = keep.tile([P, SLOTS], F32, name="gates")
+        w2_raw = keep.tile([P, E, PACK * N], F32, name="w2_raw", align_bytes=DMA_ALIGN)
+        gates = keep.tile([P, SLOTS], F32, name="gates", align_bytes=DMA_ALIGN)
 
         def load_x(s):
-            x_raw[s] = keep.tile([P, PACK * T], F32, name=f"x_raw{s}")
+            x_raw[s] = keep.tile([P, PACK * T], F32, name=f"x_raw{s}", align_bytes=DMA_ALIGN)
             rows = xT[s * K_PASS:(s + 1) * K_PASS, :].rearrange("(p j) n -> p (j n)", j=PACK)
             nc.sync.dma_start(out=x_raw[s][:], in_=rows)
 
         def load_w1(e, s):
-            w1_raw[e, s] = raws.tile([P, PACK * H], F32, name=f"w1_raw{e}{s}", tag="w1_raw", align_bytes=64)
+            w1_raw[e, s] = raws.tile(
+                [P, PACK * H], F32, name=f"w1_raw{e}{s}", tag="w1_raw", align_bytes=DMA_ALIGN
+            )
             rows = w1[e, s * K_PASS:(s + 1) * K_PASS, :].rearrange("(p j) c -> p (j c)", j=PACK)
             nc.sync.dma_start(out=w1_raw[e, s][:], in_=rows)
 
@@ -76,7 +79,7 @@ def tile_routed_moe_kernel(tc, xT, w1, w2, gate, offs, out):
         for e in (LAST - 1, LAST):
             load_gate(e, e + 1)
 
-        window = keep.tile([P, T], F32, name="window")
+        window = keep.tile([P, T], F32, name="window", align_bytes=DMA_ALIGN)
         nc.gpsimd.memset(window[:], 0.0)
         zeros = keep.tile([P, C], F32, name="zeros")
         nc.scalar.activation(zeros[:], window[:, 0:C], GELU)

@@ -80,7 +80,8 @@ def tile_routed_moe_kernel(tc, xT, w1, w2, gate, offs, out):
             load_gate(e, e + 1)
 
         window = keep.tile([P, T], F32, name="window", align_bytes=DMA_ALIGN)
-        nc.gpsimd.memset(window[:], 0.0)
+        for part in range(3):
+            nc.vector.memset(window[:, part * SLOTS:(part + 1) * SLOTS], 0.0)
         zeros = keep.tile([P, C], F32, name="zeros")
         nc.scalar.activation(zeros[:], window[:, 0:C], GELU)
 

@@ -14,7 +14,8 @@ LIST_ROWS = 16
 
 SCALAR_GROUPS = (56, 96, 80)
 SCALAR_GROUPS_FIRST_EXPERT = (P, 0, SCALAR_GROUPS[2])
-SCALAR_GROUPS_NO_SECOND_LAYER = 52
+SCALAR_GROUPS_NO_SECOND_LAYER = 44
+SCALAR_GROUPS_BEFORE_LAST_CYCLE = 68
 SCALAR_GROUPS_LAST_PASS = (56, 24)
 DMA_ALIGN = 256
 W1_RAW_BUFS = 6
@@ -175,7 +176,10 @@ def tile_routed_moe_kernel(tc, xT, w1, w2, gate, offs, out):
                     cols = slice(t * P, (t + 1) * P)
                     quantize(codes[:, cols], scales[:, cols], grouped[:, t * K_PASS:(t + 1) * K_PASS])
             else:
-                scalar_groups = SCALAR_GROUPS_NO_SECOND_LAYER if (e, s) == (LAST, 1) else SCALAR_GROUPS[s]
+                scalar_groups = {
+                    (LAST, 1): SCALAR_GROUPS_NO_SECOND_LAYER,
+                    (LAST - 1, PASSES - 1): SCALAR_GROUPS_BEFORE_LAST_CYCLE,
+                }.get((e, s), SCALAR_GROUPS[s])
                 interleave_w1(grouped[:], raw, scalar_groups, slice(0, 4))
                 quantize(codes, scales, grouped[:])
             multiply_w1(e, s, codes, scales)

from contextlib import ExitStack

import concourse.mybir as mybir

K, T, E, C, H, N = 1536, 1536, 4, 128, 512, 128
SLOTS = E * C
P = 128
PACK = 4
K_PASS = P * PACK
PASSES = K // K_PASS
FLOPS = 2 * SLOTS * (K * H + H * N)
LAST = E - 1
LIST_ROWS = 16

SCALAR_GROUPS = (56, 96, 80)
SCALAR_GROUPS_FIRST_EXPERT = (P, 0, SCALAR_GROUPS[2])
SCALAR_GROUPS_NO_SECOND_LAYER = 44
SCALAR_GROUPS_BEFORE_LAST_CYCLE = 68
SCALAR_GROUPS_LAST_PASS = (56, 24)
DMA_ALIGN = 256
W1_RAW_BUFS = 6
W1_GROUPED_BUFS = 4

F32 = mybir.dt.float32
BF16 = mybir.dt.bfloat16
U32 = mybir.dt.uint32
U16 = mybir.dt.uint16
U8 = mybir.dt.uint8
FP8X4 = mybir.dt.float8_e4m3fn_x4
GELU = mybir.ActivationFunctionType.Gelu_apprx_tanh
MULT = mybir.AluOpType.mult
ADD = mybir.AluOpType.add


def tile_routed_moe_kernel(tc, xT, w1, w2, gate, offs, out):
    nc = tc.nc
    with ExitStack() as ctx:
        keep = ctx.enter_context(tc.tile_pool(name="keep", bufs=1))
        raws = ctx.enter_context(tc.tile_pool(name="raws", bufs=W1_RAW_BUFS))
        work = ctx.enter_context(tc.tile_pool(name="work", bufs=2))
        psum = ctx.enter_context(tc.psum_pool(name="psum", bufs=1))

        offsets = keep.tile([P, SLOTS // LIST_ROWS], U16, name="offsets")
        x_raw, w1_raw = {}, {}
        w2_raw = keep.tile([P, E, PACK * N], F32, name="w2_raw", align_bytes=DMA_ALIGN)
        gates = keep.tile([P, SLOTS], F32, name="gates", align_bytes=DMA_ALIGN)

        def load_x(s):
            x_raw[s] = keep.tile([P, PACK * T], F32, name=f"x_raw{s}", align_bytes=DMA_ALIGN)
            rows = xT[s * K_PASS:(s + 1) * K_PASS, :].rearrange("(p j) n -> p (j n)", j=PACK)
            nc.sync.dma_start(out=x_raw[s][:], in_=rows)

        def load_w1(e, s):
            w1_raw[e, s] = raws.tile(
                [P, PACK * H], F32, name=f"w1_raw{e}{s}", tag="w1_raw", align_bytes=DMA_ALIGN
            )
            rows = w1[e, s * K_PASS:(s + 1) * K_PASS, :].rearrange("(p j) c -> p (j c)", j=PACK)
            nc.sync.dma_start(out=w1_raw[e, s][:], in_=rows)

        def load_w2(e):
            nc.sync.dma_start(out=w2_raw[:, e, :], in_=w2[e].rearrange("(p j) n -> p (j n)", j=PACK))

        def load_gate(first, end):
            nc.sync.dma_start(out=gates[:, first * C:end * C], in_=gate[:, first * C:end * C])

        for s in range(PASSES):
            load_x(s)
            if s == 0:
                nc.sync.dma_start(offsets[:], offs)
        for e in range(E):
            load_w1(e, 0)
            if 0 < e < LAST:
                load_w2(e - 1)
            load_w1(e, 1)
            if e == 1:
                load_gate(0, LAST - 1)
            load_w1(e, 2)
        for e in (LAST - 1, LAST):
            load_w2(e)
        for e in (LAST - 1, LAST):
            load_gate(e, e + 1)

        window = keep.tile([P, T], F32, name="window", align_bytes=DMA_ALIGN)
        for part in range(3):
            nc.vector.memset(window[:, part * SLOTS:(part + 1) * SLOTS], 0.0)
        zeros = keep.tile([P, C], F32, name="zeros")
        nc.scalar.activation(zeros[:], window[:, 0:C], GELU)

        piece_codes = keep.tile([P, 2 * PASSES, SLOTS], U32, name="piece_codes", align_bytes=64)
        piece_scales = keep.tile([P, 2 * PASSES, SLOTS], U8, name="piece_scales", align_bytes=64)
        early_pieces = 2 * PASSES - 2
        early_grouped = keep.tile([P, early_pieces, SLOTS * PACK], BF16, name="early_grouped", align_bytes=64)
        late_grouped = w1_raw[0, 0][:].bitcast(BF16).rearrange("p (a f) -> p a f", a=2)
        x_piece, w_piece = (0, 1, 4), (2, 3, 5)

        def grouped_piece(piece):
            return early_grouped[:, piece, :] if piece < early_pieces else late_grouped[:, piece - early_pieces, :]

        def quantize(codes, scales, grouped):
            nc.vector.quantize_mx(out=codes.bitcast(FP8X4), scales=scales, in_=grouped)

        def merged(ap):
            return ap.rearrange("p a f -> p (a f)")

        def quantize_pieces(first, end):
            grouped = early_grouped[:, first:end, :] if first < early_pieces else late_grouped
            quantize(merged(piece_codes[:, first:end, :]), merged(piece_scales[:, first:end, :]), merged(grouped))

        def interleave(copy, grouped, raw):
            copy(
                out=grouped.rearrange("p (c i j) -> p c j i", i=4, j=PACK),
                in_=raw.rearrange("p (j c i) -> p c j i", i=4, j=PACK),
            )

        picked = {}

        def gather_tokens(s):
            picked[s] = work.tile([P, PACK, SLOTS], F32, name=f"picked{s}", tag="picked")
            for j in range(PACK):
                nc.vector.tensor_copy(picked[s][:, j, :], x_raw[s][:, j * T:(j + 1) * T].indirect(offsets[:]))

        def interleave_tokens(s):
            interleave(nc.scalar.copy, grouped_piece(x_piece[s]), merged(picked[s][:]))

        def interleave_w1(grouped, raw, scalar_groups, t):
            for copy, m in ((nc.scalar.copy, slice(0, scalar_groups)), (nc.vector.tensor_copy, slice(scalar_groups, P))):
                if m.start < m.stop:
                    copy(
                        out=grouped.rearrange("p (t m j) -> p m j t", t=4, j=PACK)[:, m, :, t],
                        in_=raw.rearrange("p (j m t) -> p m j t", j=PACK, t=4)[:, m, :, t],
                    )

        w1_codes, w1_scales, sums = {}, {}, {}

        def per_bank(e):
            return 2 if e == LAST else 4

        def multiply_w1(e, s, codes, scales):
            slots = slice(e * C, (e + 1) * C)
            for t in range(4):
                bank, place = divmod(t, per_bank(e))
                if s == 0 and place == 0:
                    sums[e, bank] = psum.tile([P, per_bank(e), C], F32, name=f"sums{e}{bank}", tag=f"sums{e}{bank}")
                cols = slice(t * P, (t + 1) * P)
                nc.tensor.matmul_mx(
                    out=sums[e, bank][:, place, :],
                    lhsT=codes[:, cols].bitcast(FP8X4),
                    lhsT_scale=scales[:, cols],
                    rhs=piece_codes[:, x_piece[s], slots].bitcast(FP8X4),
                    rhs_scale=piece_scales[:, x_piece[s], slots],
                    start=(s == 0 and place == 0),
                    stop=(s == PASSES - 1 and place == per_bank(e) - 1),
                )

        def first_expert_pass(s):
            interleave_w1(grouped_piece(w_piece[s]), w1_raw[0, s][:], SCALAR_GROUPS_FIRST_EXPERT[s], slice(0, 4))
            if s == 0:
                interleave_tokens(PASSES - 1)
            first_piece = w_piece[s] if s == 1 else w_piece[s] - 1
            quantize_pieces(first_piece, w_piece[s] + 1)
            multiply_w1(0, s, piece_codes[:, w_piece[s], :], piece_scales[:, w_piece[s], :])

        def first_layer(e, s):
            raw = w1_raw[e, s][:]
            grouped = work.tile(
                [P, H * PACK], BF16, name=f"w1_grouped{e}{s}", tag="w1_grouped", align_bytes=64, bufs=W1_GROUPED_BUFS
            )
            if s == 0:
                w1_codes[e] = work.tile([P, PASSES, H], U32, name=f"w1_codes{e}", tag="w1_codes", align_bytes=64)
                w1_scales[e] = work.tile([P, PASSES, H], U8, name=f"w1_scales{e}", tag="w1_scales", align_bytes=64)
            codes, scales = w1_codes[e][:, s, :], w1_scales[e][:, s, :]
            if (e, s) == (LAST, PASSES - 1):
                for half, scalar_groups in enumerate(SCALAR_GROUPS_LAST_PASS):
                    interleave_w1(grouped[:], raw, scalar_groups, slice(2 * half, 2 * half + 2))
                for t in range(4):
                    cols = slice(t * P, (t + 1) * P)
                    quantize(codes[:, cols], scales[:, cols], grouped[:, t * K_PASS:(t + 1) * K_PASS])
            else:
                scalar_groups = {
                    (LAST, 1): SCALAR_GROUPS_NO_SECOND_LAYER,
                    (LAST - 1, PASSES - 1): SCALAR_GROUPS_BEFORE_LAST_CYCLE,
                }.get((e, s), SCALAR_GROUPS[s])
                interleave_w1(grouped[:], raw, scalar_groups, slice(0, 4))
                quantize(codes, scales, grouped[:])
            multiply_w1(e, s, codes, scales)

        second_grouped, ys = {}, {}

        def apply_gelu(e):
            second_grouped[e] = work.tile(
                [P, 2, C * PACK], BF16, name=f"second_grouped{e}", tag="second_grouped", align_bytes=64
            )
            for bank in range(4 // per_bank(e)):
                nc.scalar.activation(
                    second_grouped[e][:, 0, :].rearrange("p (n q t) -> p q n t", n=C, t=per_bank(e))[:, bank],
                    sums[e, bank][:].rearrange("p t n -> p n t"),
                    GELU,
                )

        def second_layer(e):
            copy = nc.scalar.copy if e >= LAST - 1 else nc.vector.tensor_copy
            interleave(copy, second_grouped[e][:, 1, :], w2_raw[:, e, :])
            codes = work.tile([P, 2, C], U32, name=f"second_codes{e}", tag="second_codes", align_bytes=64)
            scales = work.tile([P, 2, C], U8, name=f"second_scales{e}", tag="second_scales", align_bytes=64)
            for part in (slice(1, 2), slice(0, 1)) if e == LAST else (slice(0, 2),):
                quantize(merged(codes[:, part, :]), merged(scales[:, part, :]), merged(second_grouped[e][:, part, :]))
            ys[e] = psum.tile([P, C], F32, name=f"y{e}", tag=f"y{e % 2}")
            nc.tensor.matmul_mx(
                out=ys[e][:],
                lhsT=codes[:, 1, :].bitcast(FP8X4),
                lhsT_scale=scales[:, 1, :],
                rhs=codes[:, 0, :].bitcast(FP8X4),
                rhs_scale=scales[:, 0, :],
                start=True,
                stop=True,
            )

        def put_back(e):
            if e == 1:
                gated = w1_raw[e + 1, 1][:, PACK * H - C:]
            else:
                gated_tile = work.tile([P, C], F32, name=f"gated{e}", tag="gated")
                gated = gated_tile[:]
            nc.vector.tensor_tensor(gated, ys[e][:], gates[:, e * C:(e + 1) * C], MULT)
            entries = slice(e * C // LIST_ROWS, (e + 1) * C // LIST_ROWS)
            nc.vector.tensor_tensor(window[:].indirect(offsets[:, entries]), gated, zeros[:], ADD)

        for s in range(PASSES):
            gather_tokens(s)
            if s < PASSES - 1:
                interleave_tokens(s)
            if s == 0:
                quantize_pieces(0, 1)
        for s in range(PASSES):
            first_expert_pass(s)
        apply_gelu(0)
        for e in range(1, E):
            first_layer(e, 0)
            if e < LAST:
                second_layer(e - 1)
            first_layer(e, 1)
            if e < LAST:
                put_back(e - 1)
            first_layer(e, 2)
            if e == LAST:
                second_layer(e - 1)
                put_back(e - 1)
            apply_gelu(e)
        second_layer(LAST)
        put_back(LAST)
        nc.sync.dma_start(out=out, in_=window[:])
